import numpy as np
import ml_dtypes


def mxq(x, axis, fmt="e4m3"):
    dtype, down = {"e4m3": (ml_dtypes.float8_e4m3fn, 7), "e5m2": (ml_dtypes.float8_e5m2, 14)}[fmt]
    v = np.moveaxis(np.asarray(x, np.float32).astype(ml_dtypes.bfloat16).astype(np.float64), axis, -1)
    blocks = v.reshape(v.shape[:-1] + (-1, 32))
    amax = np.abs(blocks).max(-1, keepdims=True)
    byte = np.maximum(np.where(amax > 0, np.frexp(amax)[1] - 1 + 127, 0) - down, 1)
    scale = np.exp2(byte - 127.0)
    codes = (blocks / scale).astype(np.float32).astype(dtype).astype(np.float64)
    return np.moveaxis((codes * scale).reshape(v.shape), -1, axis)


WIDE = False


def mx_kscale(k):
    if not WIDE:
        return np.ones(k)
    levels = np.array([10, -10, 5, -5, 0])
    if k % 512:
        return np.exp2(np.random.permutation(np.resize(levels, k // 32))).repeat(32)
    a = np.empty((k // 512, 16))
    for p in range(k // 512):
        a[p, :8] = np.random.permutation(np.resize(levels, 8))
        for g in range(8):
            far = levels[np.abs(levels - a[p, g]) >= 10]
            a[p, g + 8] = far[np.random.randint(len(far))]
    return np.exp2(a.ravel()).repeat(32)


def f64(x):
    return np.asarray(x).astype(np.float64)


def striped(idx):
    return np.tile(idx.reshape(-1, 16).T, (8, 1)).astype(np.uint16)


def unstriped(offs):
    return offs[:16].T.reshape(-1).astype(np.int64)


def striped8(idx):
    return np.concatenate([x.reshape(-1, 16).T for x in idx]).astype(np.uint16)


def runs(offs, k):
    lists = np.stack([offs[16 * r : 16 * r + 16].T.reshape(-1) for r in range(8)]).astype(np.int64)
    return lists[np.arange(k) % 512 // 64]


def pack_weight(w):
    k, n = w.shape
    w = f64(np.asarray(w, np.float32).astype(ml_dtypes.bfloat16)).reshape(k // 32, 32, n)
    amax = np.abs(w).max(1)
    byte = np.clip(np.where(amax > 0, np.frexp(amax)[1] - 1 + 127 - 7, 1), 1, 254)
    scaled = (w * np.exp2(127.0 - byte)[:, None, :]).reshape(k, n).astype(np.float32)
    words = np.ascontiguousarray(scaled.reshape(k // 512, 128, 4, n).transpose(0, 1, 3, 2)).astype(ml_dtypes.float8_e4m3fn).view(np.uint8)
    return words, np.ascontiguousarray(byte.astype(np.uint8).reshape(k // 512, 16, n))


def unpack_weight(words, scales):
    g, p, n, _ = words.shape
    vals = np.ascontiguousarray(words).view(ml_dtypes.float8_e4m3fn).astype(np.float64) * np.repeat(np.exp2(scales.astype(np.float64) - 127.0), 8, axis=1)[..., None]
    return vals.transpose(0, 1, 3, 2).reshape(g * 512, n)


def sigmoid(v):
    return 1.0 / (1.0 + np.exp(-np.maximum(v, -700.0)))


K, T, S, N, H = 512, 2048, 512, 512, 512


def setup_inputs():
    n = np.random.standard_normal
    s = mx_kscale(K)[:, None]
    u = mx_kscale(H)
    packed_xT = pack_weight(n((K, T)) * s)
    return {
        "x_words": packed_xT[0],
        "x_scales": packed_xT[1],
        "w1": (n((K, H)) / np.sqrt(K) / s).astype(np.float32),
        "w2": (n((K, H)) / np.sqrt(K) / s).astype(np.float32),
        "sl": np.random.uniform(1.0, 2.0, (H, 1)).astype(np.float32),
        "th": (0.5 * n((H, 1))).astype(np.float32),
        "gn": (np.random.uniform(0.5, 1.5, (H, 1)) * u[:, None]).astype(np.float32),
        "w3": (n((H, N)) / np.sqrt(H) / u[:, None]).astype(np.float32),
        "tau": np.random.uniform(0.3, 0.9, (N, 1)).astype(np.float32),
        "offs": striped(np.random.permutation(T)[:S]),
        "hz": striped8(np.random.randint(0, T, (8, S))),
        "n1": striped(np.random.permutation(S)),
        "n2": striped(np.random.permutation(S)),
        "n3": striped8(np.stack([np.random.permutation(S) for _ in range(8)])),
        "n4": striped8(np.stack([np.random.permutation(S) for _ in range(8)])),
    }


def reference(x_words, x_scales, w1, w2, sl, th, gn, w3, tau, offs, hz, n1, n2, n3, n4):
    xq = unpack_weight(x_words, x_scales)[:, unstriped(offs)]
    y = mxq(f64(w1), 0, "e4m3").T @ xq
    x_hz = unpack_weight(x_words, x_scales)[np.arange(K)[:, None], runs(hz, K)]
    d = mxq(f64(w2), 0, "e4m3").T @ x_hz
    sg = sigmoid(f64(sl) * (d[:, unstriped(n1)] - f64(th)))
    z = f64(gn) * (y * sg - (0.5 * y[:, unstriped(n2)]))
    h = mxq(f64(w3), 0, "e4m3").T @ mxq(z, 0, "e4m3")
    top = h.max(axis=1, keepdims=True)
    ea = np.exp(f64(tau) * (h[np.arange(N)[:, None], runs(n3, N)] - top))
    ea2 = np.exp(f64(tau) * (h[np.arange(N)[:, None], runs(n4, N)] - top))
    return h + np.log(ea + ea2 + 0.25)

@@ -1,0 +1,197 @@
+from contextlib import ExitStack
+
+import concourse.mybir as mybir
+
+K, T, S, N, H = 512, 2048, 512, 512, 512
+FLOPS = 3 * 2 * 512 * 512 * 512
+
+F32 = mybir.dt.float32
+BF16 = mybir.dt.bfloat16
+I32 = mybir.dt.int32
+U32 = mybir.dt.uint32
+U16 = mybir.dt.uint16
+U8 = mybir.dt.uint8
+FP8X4 = mybir.dt.float8_e4m3fn_x4
+ALU = mybir.AluOpType
+ACT = mybir.ActivationFunctionType
+
+P = 128
+PACK = 4
+STRIPE = 16
+PIECES = ((0, 256), (256, 384), (384, 512))
+HALF = 256
+
+
+def tile_picked_twhgxbelg_none_p_kernel(tc, x_words, x_scales, w1, w2, sl, th, gn, w3, tau, offs, hz, n1, n2, n3, n4, out):
+    nc = tc.nc
+    with ExitStack() as ctx:
+        keep = ctx.enter_context(tc.tile_pool(name="keep", bufs=1))
+        psum = ctx.enter_context(tc.psum_pool(name="psum", bufs=1))
+
+        def load_list(src, name):
+            tile = keep.tile([P, S // STRIPE], U16, name=name)
+            nc.sync.dma_start(tile[:], src)
+            return tile
+
+        def entries(tile, lo, hi):
+            return tile[:, lo // STRIPE : hi // STRIPE]
+
+        def load_weight(w, name, tag):
+            raw = keep.tile([P, PACK, w.shape[1]], F32, name=name, tag=tag)
+            nc.sync.dma_start(raw[:], w.rearrange("(p j) c -> p j c", j=PACK))
+            return raw
+
+        def load_column(vec, name):
+            tile = keep.tile([P, PACK], F32, name=name)
+            nc.gpsimd.dma_start(tile[:], vec.rearrange("(p t) o -> p (t o)", t=PACK))
+            return tile
+
+        def dealt(raw, rounded, lo, hi):
+            dst = rounded[:].rearrange("p (t m j) -> p m j t", t=PACK, j=PACK)[:, lo:hi]
+            src = raw[:].rearrange("p j (m t) -> p m j t", t=PACK)[:, lo:hi]
+            return dst, src
+
+        def quantise(rounded, codes, plane, lo, hi):
+            nc.vector.quantize_mx(out=codes[:, lo:hi].bitcast(FP8X4), scales=plane[:, lo:hi], in_=rounded[:, PACK * lo : PACK * hi])
+
+        def product(acc, codes, plane, t, rhs, rhs_plane):
+            cols = slice(P * t, P * (t + 1))
+            nc.tensor.matmul_mx(out=acc, lhsT=codes[:, cols].bitcast(FP8X4), lhsT_scale=plane[:, cols], rhs=rhs.bitcast(FP8X4), rhs_scale=rhs_plane, start=True, stop=True)
+
+        def weight_tiles(name):
+            rounded = keep.tile([P, PACK * H], BF16, name=name + "_rounded", align_bytes=64)
+            codes = keep.tile([P, H], U32, name=name + "_codes", align_bytes=64)
+            plane = keep.tile([P, H], U8, name=name + "_plane", align_bytes=64)
+            return rounded, codes, plane
+
+        scale_table = keep.tile([P, T], U8, name="scale_table", tag="bytes_then_words", align_bytes=64)
+        nc.vector.memset(scale_table[:].bitcast(I32), 0)
+        hz_l = load_list(hz, "hz_l")
+        offs_l = load_list(offs, "offs_l")
+        n1_l = load_list(n1, "n1_l")
+        n2_l = load_list(n2, "n2_l")
+        scale_rows = x_scales[0].rearrange("(g e) n -> e g n", e=2)
+        for e in range(2):
+            nc.scalar.dma_start(scale_table[e:P:STRIPE, :].bitcast(I32), scale_rows[e].bitcast(I32))
+        word_table = keep.tile([P, T], I32, name="word_table", align_bytes=64)
+        nc.sync.dma_start(word_table[:], x_words[0].rearrange("p n r -> p (n r)").bitcast(I32))
+        w2_raw = [load_weight(w2[:, HALF * u : HALF * (u + 1)], "w2_raw%d" % u, "raw_a" if u else "raw_c") for u in range(2)]
+        w1_raw = load_weight(w1, "w1_raw", "raw_b")
+        n3_l = load_list(n3, "n3_l")
+        n4_l = load_list(n4, "n4_l")
+        sl_c = load_column(sl, "sl_c")
+        th_c = load_column(th, "th_c")
+        gn_c = load_column(gn, "gn_c")
+        tau_c = load_column(tau, "tau_c")
+        sl_th = keep.tile([P, PACK], F32, name="sl_th")
+        nc.gpsimd.tensor_tensor(sl_th[:], sl_c[:], th_c[:], ALU.mult)
+        sig_bias = keep.tile([P, PACK], F32, name="sig_bias")
+        nc.gpsimd.tensor_scalar(sig_bias[:], sl_th[:], -1.0, 0.0, ALU.mult, ALU.add)
+
+        picked_scales = keep.tile([P, 2 * S], U8, name="picked_scales", align_bytes=64)
+        nc.vector.tensor_copy(picked_scales[:, 0:S], scale_table[:].indirect(hz_l[:]))
+        nc.vector.tensor_copy(picked_scales[:, S : 2 * S], scale_table[:].indirect(offs_l[:]))
+        x_plane = keep.tile([P, 2 * S], U8, name="x_plane", align_bytes=64)
+        nc.vector.tensor_copy(x_plane[:].bitcast(I32), picked_scales[:].bitcast(I32))
+        for e in range(2):
+            nc.scalar.dma_start(x_plane[2 + e : P : 32, :].bitcast(I32), picked_scales[STRIPE + e : P : 32, :].bitcast(I32))
+        picked_words = keep.tile([P, 2 * S], U32, name="picked_words", tag="bytes_then_words", align_bytes=64)
+        hz_words, offs_words = picked_words[:, 0:S], picked_words[:, S : 2 * S]
+        nc.vector.tensor_copy(hz_words, word_table[:].bitcast(U32).indirect(hz_l[:]))
+        nc.vector.tensor_copy(offs_words, word_table[:].bitcast(U32).indirect(offs_l[:]))
+
+        w2_rounded = [keep.tile([P, PACK * HALF], BF16, name="w2_rounded%d" % u, align_bytes=64) for u in range(2)]
+        w2_codes = keep.tile([P, H], U32, name="w2_codes", align_bytes=64)
+        w2_plane = keep.tile([P, H], U8, name="w2_plane", align_bytes=64)
+        for u in range(2):
+            nc.scalar.copy(*dealt(w2_raw[u], w2_rounded[u], 0, P // 2))
+        d_acc = [psum.tile([P, S], F32, name="d_acc%d" % t, tag="bank%d" % t) for t in range(PACK)]
+        d_rows = [keep.tile([P, S], F32, name="d_rows%d" % t) for t in range(PACK)]
+        last = PACK - 1
+        h_rows = [keep.tile([P, (PACK if t == last else 2) * S], F32, name="h_rows%d" % t) for t in range(PACK)]
+        sg_last = keep.tile([P, S], F32, name="sg_last")
+        sg = [h_rows[t][:, S : 2 * S] for t in range(last)] + [sg_last[:]]
+        for t in range(PACK):
+            for u in range(2):
+                cols = slice(P * t + 64 * u, P * t + 64 * (u + 1))
+                nc.vector.quantize_mx(out=w2_codes[:, cols].bitcast(FP8X4), scales=w2_plane[:, cols], in_=w2_rounded[u][:, HALF * t : HALF * (t + 1)])
+            product(d_acc[t][:], w2_codes, w2_plane, t, hz_words, x_plane[:, 0:S])
+        w3_raw = load_weight(w3, "w3_raw", "raw_a")
+
+        def sigmoid(t):
+            for lo in range(0, S, S // 2):
+                hi = lo + S // 2
+                nc.scalar.activation(sg[t][:, lo:hi], d_rows[t][:].indirect(entries(n1_l, lo, hi)), ACT.Sigmoid, bias=sig_bias[:, t : t + 1], scale=sl_c[:, t : t + 1])
+
+        w1_rounded, w1_codes, w1_plane = weight_tiles("w1")
+        y_acc = [psum.tile([P, S], F32, name="y_acc%d" % t, tag="bank%d" % (PACK + t)) for t in range(PACK)]
+        y_rows = [keep.tile([P, S], F32, name="y_rows%d" % t) for t in range(PACK)]
+
+        nc.scalar.copy(d_rows[0][:], d_acc[0][:])
+        sigmoid(0)
+        nc.scalar.copy(d_rows[1][:], d_acc[1][:])
+        sigmoid(1)
+        nc.vector.tensor_copy(*dealt(w1_raw, w1_rounded, 0, P))
+        for half in range(2):
+            quantise(w1_rounded, w1_codes, w1_plane, 2 * P * half, 2 * P * (half + 1))
+        for t in range(PACK):
+            product(y_acc[t][:], w1_codes, w1_plane, t, offs_words, x_plane[:, S : 2 * S])
+        nc.scalar.copy(d_rows[2][:], d_acc[2][:])
+        sigmoid(2)
+        nc.scalar.copy(d_rows[3][:], d_acc[3][:])
+        sigmoid(3)
+        for t in range(PACK):
+            nc.vector.tensor_scalar(y_rows[t][:], y_acc[t][:], gn_c[:, t : t + 1], -0.5, ALU.mult, ALU.mult)
+
+        w3_rounded, w3_codes, w3_plane = weight_tiles("w3")
+        nc.vector.tensor_copy(*dealt(w3_raw, w3_rounded, 0, P))
+
+        fetched_last = keep.tile([P, S], F32, name="fetched_last")
+        fetched_flat = [h_rows[last][:, S : 3 * S], h_rows[last][:, 3 * S : 4 * S], fetched_last[:]]
+        fetched = [flat.rearrange("p (t c) -> p t c", t=PACK) for flat in fetched_flat]
+        gated = keep.tile([P, PACK, S], F32, name="gated")
+        for t in range(PACK):
+            nc.vector.scalar_tensor_tensor(gated[:, t, :], y_acc[t][:], gn_c[:, t : t + 1], sg[t], ALU.mult, ALU.mult)
+        z_rounded = keep.tile([P, PACK * S], BF16, name="z_rounded", align_bytes=64)
+        z_codes = keep.tile([P, S], U32, name="z_codes", align_bytes=64)
+        z_plane = keep.tile([P, S], U8, name="z_plane", align_bytes=64)
+        h_acc = [psum.tile([P, S], F32, name="h_acc%d" % t, tag="bank%d" % t) for t in range(PACK)]
+        for i, (lo, hi) in enumerate(PIECES):
+            for t in range(PACK):
+                nc.scalar.activation(fetched[i][:, t, :], y_rows[t][:].indirect(entries(n2_l, lo, hi)), ACT.Copy)
+        quantise(w3_rounded, w3_codes, w3_plane, 0, N)
+        for i, (lo, hi) in enumerate(PIECES):
+            nc.vector.tensor_tensor(
+                z_rounded[:, PACK * lo : PACK * hi].rearrange("p (c i t) -> p c t i", i=4, t=PACK),
+                gated[:, :, lo:hi].rearrange("p t (c i) -> p c t i", i=4),
+                fetched[i].rearrange("p t (c i) -> p c t i", i=4),
+                ALU.add,
+            )
+            quantise(z_rounded, z_codes, z_plane, lo, hi)
+            for t in range(PACK):
+                product(h_acc[t][:, lo:hi], w3_codes, w3_plane, t, z_codes[:, lo:hi], z_plane[:, lo:hi])
+
+        top = keep.tile([P, PACK], F32, name="top")
+        exp_bias = keep.tile([P, PACK], F32, name="exp_bias")
+        total = [keep.tile([P, S], F32, name="total%d" % t) for t in range(PACK)]
+        for t in range(PACK):
+            col = slice(t, t + 1)
+            nc.vector.tensor_scalar(h_rows[t][:, 0:S], h_acc[t][:], 1.0, None, ALU.mult, ALU.max, accum_out=top[:, col])
+            nc.vector.tensor_scalar(exp_bias[:, col], top[:, col], tau_c[:, col], -1.0, ALU.mult, ALU.mult)
+        for t in range(PACK):
+            col = slice(t, t + 1)
+            ea = keep.tile([P, S], F32, name="ea%d" % t)
+            ea2 = keep.tile([P, S], F32, name="ea2_%d" % t)
+            nc.scalar.activation(ea[:], h_rows[t][:].indirect(n3_l[:]), ACT.Exp, bias=exp_bias[:, col], scale=tau_c[:, col])
+            nc.scalar.activation(ea2[:], h_rows[t][:].indirect(n4_l[:]), ACT.Exp, bias=exp_bias[:, col], scale=tau_c[:, col])
+            nc.vector.scalar_tensor_tensor(total[t][:], ea[:], 0.25, ea2[:], ALU.add, ALU.add)
+        out_rows = out.rearrange("(p t) s -> t p s", t=PACK)
+        for t in range(PACK):
+            logs = h_rows[last][:, S * (t + 1) : S * (t + 2)] if t < last else sg_last[:]
+            result = keep.tile([P, S], F32, name="result%d" % t)
+            step = S // 2 if t == last else S
+            for lo in range(0, S, step):
+                cols = slice(lo, lo + step)
+                nc.scalar.activation(logs[:, cols], total[t][:, cols], ACT.Ln)
+                nc.vector.tensor_tensor(result[:, cols], h_rows[t][:, cols], logs[:, cols], ALU.add)
+                nc.sync.dma_start(out_rows[t][:, cols], result[:, cols])

@@ -64,6 +64,11 @@ def tile_picked_twhgxbelg_none_p_kernel(tc, x_words, x_scales, w1, w2, sl, th, g
             plane = keep.tile([P, H], U8, name=name + "_plane", align_bytes=64)
             return rounded, codes, plane
 
+        warm_in = keep.tile([P, 1], F32, name="warm_in")
+        warm_out = keep.tile([P, 1], F32, name="warm_out")
+        nc.gpsimd.memset(warm_in[:], 0.0)
+        nc.scalar.activation(warm_out[:], warm_in[:], ACT.Sigmoid)
+
         scale_table = keep.tile([P, T], U8, name="scale_table", tag="bytes_then_words", align_bytes=64)
         nc.vector.memset(scale_table[:].bitcast(I32), 0)
         hz_l = load_list(hz, "hz_l")

@@ -18,7 +18,7 @@ ACT = mybir.ActivationFunctionType
 P = 128
 PACK = 4
 STRIPE = 16
-PIECES = ((0, 256), (256, 384), (384, 512))
+CUTS = (128, 384)
 HALF = 256
 
 
@@ -37,18 +37,23 @@ def tile_picked_twhgxbelg_none_p_kernel(tc, x_words, x_scales, w1, w2, sl, th, g
             return tile[:, lo // STRIPE : hi // STRIPE]
 
         def load_weight(w, name, tag):
-            raw = keep.tile([P, PACK, w.shape[1]], F32, name=name, tag=tag)
-            nc.sync.dma_start(raw[:], w.rearrange("(p j) c -> p j c", j=PACK))
-            return raw
+            tile = keep.tile([P, PACK * w.shape[1]], F32, name=name, tag=tag, align_bytes=64)
+            nc.sync.dma_start(by_row(tile), w.rearrange("(p j) c -> p j c", j=PACK))
+            return tile
+
+        def by_row(tile):
+            return tile[:].rearrange("p (j c) -> p j c", j=PACK)
 
         def load_column(vec, name):
             tile = keep.tile([P, PACK], F32, name=name)
             nc.gpsimd.dma_start(tile[:], vec.rearrange("(p t) o -> p (t o)", t=PACK))
             return tile
 
-        def dealt(raw, rounded, lo, hi):
+        def dealt(raw, rounded, first_column):
+            lo = first_column // PACK
+            hi = lo + raw.shape[1] // (PACK * PACK)
             dst = rounded[:].rearrange("p (t m j) -> p m j t", t=PACK, j=PACK)[:, lo:hi]
-            src = raw[:].rearrange("p j (m t) -> p m j t", t=PACK)[:, lo:hi]
+            src = raw[:].rearrange("p (j m t) -> p m j t", j=PACK, t=PACK)
             return dst, src
 
         def quantise(rounded, codes, plane, lo, hi):
@@ -59,7 +64,7 @@ def tile_picked_twhgxbelg_none_p_kernel(tc, x_words, x_scales, w1, w2, sl, th, g
             nc.tensor.matmul_mx(out=acc, lhsT=codes[:, cols].bitcast(FP8X4), lhsT_scale=plane[:, cols], rhs=rhs.bitcast(FP8X4), rhs_scale=rhs_plane, start=True, stop=True)
 
         def weight_tiles(name):
-            rounded = keep.tile([P, PACK * H], BF16, name=name + "_rounded", align_bytes=64)
+            rounded = keep.tile([P, PACK * H], BF16, name=name + "_rounded", tag=name + "_rounded", align_bytes=64)
             codes = keep.tile([P, H], U32, name=name + "_codes", align_bytes=64)
             plane = keep.tile([P, H], U8, name=name + "_plane", align_bytes=64)
             return rounded, codes, plane
@@ -69,20 +74,23 @@ def tile_picked_twhgxbelg_none_p_kernel(tc, x_words, x_scales, w1, w2, sl, th, g
         nc.gpsimd.memset(warm_in[:], 0.0)
         nc.scalar.activation(warm_out[:], warm_in[:], ACT.Sigmoid)
 
-        scale_table = keep.tile([P, T], U8, name="scale_table", tag="bytes_then_words", align_bytes=64)
+        scale_table = keep.tile([P, T], U8, name="scale_table", tag="table_then_w1", align_bytes=64)
         nc.vector.memset(scale_table[:].bitcast(I32), 0)
+        hz_plane = keep.tile([P, S], U8, name="hz_plane", align_bytes=64)
+        offs_plane = keep.tile([P, S], U8, name="offs_plane", align_bytes=64)
+        nc.vector.memset(hz_plane[:].bitcast(I32), 0)
+        nc.vector.memset(offs_plane[:].bitcast(I32), 0)
+        nc.sync.dma_start(scale_table[0:P:8, :].bitcast(I32), x_scales[0].bitcast(I32))
         hz_l = load_list(hz, "hz_l")
+        w2_raw = [load_weight(w2[:, 0:HALF], "w2_raw0", "w2_raw0")]
         offs_l = load_list(offs, "offs_l")
         n1_l = load_list(n1, "n1_l")
         n2_l = load_list(n2, "n2_l")
-        scale_rows = x_scales[0].rearrange("(g e) n -> e g n", e=2)
-        for e in range(2):
-            nc.scalar.dma_start(scale_table[e:P:STRIPE, :].bitcast(I32), scale_rows[e].bitcast(I32))
+        n3_l = load_list(n3, "n3_l")
         word_table = keep.tile([P, T], I32, name="word_table", align_bytes=64)
         nc.sync.dma_start(word_table[:], x_words[0].rearrange("p n r -> p (n r)").bitcast(I32))
-        w2_raw = [load_weight(w2[:, HALF * u : HALF * (u + 1)], "w2_raw%d" % u, "raw_a" if u else "raw_c") for u in range(2)]
-        w1_raw = load_weight(w1, "w1_raw", "raw_b")
-        n3_l = load_list(n3, "n3_l")
+        w2_raw.append(load_weight(w2[:, HALF:H], "w2_raw1", "w2_raw1"))
+        w1_raw = [load_weight(w1[:, 0:HALF], "w1_raw0", "w1_raw0")]
         n4_l = load_list(n4, "n4_l")
         sl_c = load_column(sl, "sl_c")
         th_c = load_column(th, "th_c")
@@ -93,88 +101,116 @@ def tile_picked_twhgxbelg_none_p_kernel(tc, x_words, x_scales, w1, w2, sl, th, g
         sig_bias = keep.tile([P, PACK], F32, name="sig_bias")
         nc.gpsimd.tensor_scalar(sig_bias[:], sl_th[:], -1.0, 0.0, ALU.mult, ALU.add)
 
-        picked_scales = keep.tile([P, 2 * S], U8, name="picked_scales", align_bytes=64)
-        nc.vector.tensor_copy(picked_scales[:, 0:S], scale_table[:].indirect(hz_l[:]))
-        nc.vector.tensor_copy(picked_scales[:, S : 2 * S], scale_table[:].indirect(offs_l[:]))
-        x_plane = keep.tile([P, 2 * S], U8, name="x_plane", align_bytes=64)
-        nc.vector.tensor_copy(x_plane[:].bitcast(I32), picked_scales[:].bitcast(I32))
-        for e in range(2):
-            nc.scalar.dma_start(x_plane[2 + e : P : 32, :].bitcast(I32), picked_scales[STRIPE + e : P : 32, :].bitcast(I32))
-        picked_words = keep.tile([P, 2 * S], U32, name="picked_words", tag="bytes_then_words", align_bytes=64)
-        hz_words, offs_words = picked_words[:, 0:S], picked_words[:, S : 2 * S]
-        nc.vector.tensor_copy(hz_words, word_table[:].bitcast(U32).indirect(hz_l[:]))
-        nc.vector.tensor_copy(offs_words, word_table[:].bitcast(U32).indirect(offs_l[:]))
+        def move_rows(plane, picked):
+            for a in range(4):
+                nc.sync.dma_start(plane[a:P:32, :].bitcast(I32), picked[8 * a : P : 32, :].bitcast(I32))
 
-        w2_rounded = [keep.tile([P, PACK * HALF], BF16, name="w2_rounded%d" % u, align_bytes=64) for u in range(2)]
-        w2_codes = keep.tile([P, H], U32, name="w2_codes", align_bytes=64)
-        w2_plane = keep.tile([P, H], U8, name="w2_plane", align_bytes=64)
+        hz_scales = keep.tile([P, S], U8, name="hz_scales", align_bytes=64)
+        offs_scales = keep.tile([P, S], U8, name="offs_scales", align_bytes=64)
+        nc.vector.tensor_copy(hz_scales[:], scale_table[:].indirect(hz_l[:]))
+        move_rows(hz_plane, hz_scales)
+        nc.vector.tensor_copy(offs_scales[:], scale_table[:].indirect(offs_l[:]))
+        w1_raw.append(load_weight(w1[:, HALF:H], "w1_raw1", "table_then_w1"))
+        move_rows(offs_plane, offs_scales)
+
+        hz_words = keep.tile([P, S], U32, name="hz_words", align_bytes=64)
+        nc.vector.tensor_copy(hz_words[:], word_table[:].bitcast(U32).indirect(hz_l[:]))
+        offs_words = keep.tile([P, S], U32, name="offs_words", align_bytes=64)
+        nc.vector.tensor_copy(offs_words[:], word_table[:].bitcast(U32).indirect(offs_l[:]))
+
+        w2_rounded, w2_codes, w2_plane = weight_tiles("w2")
         for u in range(2):
-            nc.scalar.copy(*dealt(w2_raw[u], w2_rounded[u], 0, P // 2))
+            nc.scalar.copy(*dealt(w2_raw[u], w2_rounded, HALF * u))
+        quantise(w2_rounded, w2_codes, w2_plane, 0, P)
+        quantise(w2_rounded, w2_codes, w2_plane, P, H)
+        w3_raw = load_weight(w3, "w3_raw", "w2_rounded")
         d_acc = [psum.tile([P, S], F32, name="d_acc%d" % t, tag="bank%d" % t) for t in range(PACK)]
-        d_rows = [keep.tile([P, S], F32, name="d_rows%d" % t) for t in range(PACK)]
+        d_rows = w2_raw + w1_raw
         last = PACK - 1
         h_rows = [keep.tile([P, (PACK if t == last else 2) * S], F32, name="h_rows%d" % t) for t in range(PACK)]
         sg_last = keep.tile([P, S], F32, name="sg_last")
         sg = [h_rows[t][:, S : 2 * S] for t in range(last)] + [sg_last[:]]
         for t in range(PACK):
-            for u in range(2):
-                cols = slice(P * t + 64 * u, P * t + 64 * (u + 1))
-                nc.vector.quantize_mx(out=w2_codes[:, cols].bitcast(FP8X4), scales=w2_plane[:, cols], in_=w2_rounded[u][:, HALF * t : HALF * (t + 1)])
-            product(d_acc[t][:], w2_codes, w2_plane, t, hz_words, x_plane[:, 0:S])
-        w3_raw = load_weight(w3, "w3_raw", "raw_a")
+            product(d_acc[t][:], w2_codes, w2_plane, t, hz_words[:], hz_plane[:])
 
         def sigmoid(t):
-            for lo in range(0, S, S // 2):
-                hi = lo + S // 2
-                nc.scalar.activation(sg[t][:, lo:hi], d_rows[t][:].indirect(entries(n1_l, lo, hi)), ACT.Sigmoid, bias=sig_bias[:, t : t + 1], scale=sl_c[:, t : t + 1])
+            nc.scalar.activation(sg[t], d_rows[t][:].indirect(n1_l[:]), ACT.Sigmoid, bias=sig_bias[:, t : t + 1], scale=sl_c[:, t : t + 1])
 
         w1_rounded, w1_codes, w1_plane = weight_tiles("w1")
         y_acc = [psum.tile([P, S], F32, name="y_acc%d" % t, tag="bank%d" % (PACK + t)) for t in range(PACK)]
         y_rows = [keep.tile([P, S], F32, name="y_rows%d" % t) for t in range(PACK)]
 
-        nc.scalar.copy(d_rows[0][:], d_acc[0][:])
+        nc.scalar.copy(*dealt(w1_raw[0], w1_rounded, 0))
+        nc.scalar.copy(d_rows[0][:, 0:S], d_acc[0][:])
         sigmoid(0)
-        nc.scalar.copy(d_rows[1][:], d_acc[1][:])
+        nc.scalar.copy(d_rows[1][:, 0:S], d_acc[1][:])
         sigmoid(1)
-        nc.vector.tensor_copy(*dealt(w1_raw, w1_rounded, 0, P))
-        for half in range(2):
-            quantise(w1_rounded, w1_codes, w1_plane, 2 * P * half, 2 * P * (half + 1))
+        nc.vector.tensor_copy(*dealt(w1_raw[1], w1_rounded, HALF))
+        quantise(w1_rounded, w1_codes, w1_plane, 0, P)
+        quantise(w1_rounded, w1_codes, w1_plane, P, H)
         for t in range(PACK):
-            product(y_acc[t][:], w1_codes, w1_plane, t, offs_words, x_plane[:, S : 2 * S])
-        nc.scalar.copy(d_rows[2][:], d_acc[2][:])
+            product(y_acc[t][:], w1_codes, w1_plane, t, offs_words[:], offs_plane[:])
+        nc.scalar.copy(d_rows[2][:, 0:S], d_acc[2][:])
         sigmoid(2)
-        nc.scalar.copy(d_rows[3][:], d_acc[3][:])
+        nc.scalar.copy(d_rows[3][:, 0:S], d_acc[3][:])
         sigmoid(3)
         for t in range(PACK):
             nc.vector.tensor_scalar(y_rows[t][:], y_acc[t][:], gn_c[:, t : t + 1], -0.5, ALU.mult, ALU.mult)
 
         w3_rounded, w3_codes, w3_plane = weight_tiles("w3")
-        nc.vector.tensor_copy(*dealt(w3_raw, w3_rounded, 0, P))
+        for t in range(PACK):
+            nc.gpsimd.tensor_scalar(
+                w3_rounded[:, N * t : N * (t + 1)].rearrange("p (m j) -> p m j", j=PACK),
+                w3_raw[:].rearrange("p (j m t) -> p t m j", j=PACK, t=PACK)[:, t],
+                1.0,
+                0.0,
+                ALU.mult,
+                ALU.add,
+            )
 
-        fetched_last = keep.tile([P, S], F32, name="fetched_last")
-        fetched_flat = [h_rows[last][:, S : 3 * S], h_rows[last][:, 3 * S : 4 * S], fetched_last[:]]
-        fetched = [flat.rearrange("p (t c) -> p t c", t=PACK) for flat in fetched_flat]
         gated = keep.tile([P, PACK, S], F32, name="gated")
         for t in range(PACK):
             nc.vector.scalar_tensor_tensor(gated[:, t, :], y_acc[t][:], gn_c[:, t : t + 1], sg[t], ALU.mult, ALU.mult)
-        z_rounded = keep.tile([P, PACK * S], BF16, name="z_rounded", align_bytes=64)
+        quantise(w3_rounded, w3_codes, w3_plane, 0, N)
+        h_acc = [psum.tile([P, S], F32, name="h_acc%d" % t, tag="bank%d" % t) for t in range(PACK)]
+
+        def woven(rounded):
+            return rounded[:].rearrange("p (c i t) -> p c t i", i=4, t=PACK)
+
+        def in_fours(planes):
+            return planes.rearrange("p t (c i) -> p c t i", i=4)
+
         z_codes = keep.tile([P, S], U32, name="z_codes", align_bytes=64)
         z_plane = keep.tile([P, S], U8, name="z_plane", align_bytes=64)
-        h_acc = [psum.tile([P, S], F32, name="h_acc%d" % t, tag="bank%d" % t) for t in range(PACK)]
-        for i, (lo, hi) in enumerate(PIECES):
+
+        def third_product(rounded, lo, hi):
+            nc.vector.quantize_mx(out=z_codes[:, lo:hi].bitcast(FP8X4), scales=z_plane[:, lo:hi], in_=rounded[:])
+            product(h_acc[0][:, lo:hi], w3_codes, w3_plane, 0, z_codes[:, lo:hi], z_plane[:, lo:hi])
+
+        def fetch_on_scalar(lo, hi):
+            planes = h_rows[last][:, PACK * lo : PACK * hi].rearrange("p (t c) -> p t c", t=PACK)
             for t in range(PACK):
-                nc.scalar.activation(fetched[i][:, t, :], y_rows[t][:].indirect(entries(n2_l, lo, hi)), ACT.Copy)
-        quantise(w3_rounded, w3_codes, w3_plane, 0, N)
-        for i, (lo, hi) in enumerate(PIECES):
-            nc.vector.tensor_tensor(
-                z_rounded[:, PACK * lo : PACK * hi].rearrange("p (c i t) -> p c t i", i=4, t=PACK),
-                gated[:, :, lo:hi].rearrange("p t (c i) -> p c t i", i=4),
-                fetched[i].rearrange("p t (c i) -> p c t i", i=4),
-                ALU.add,
-            )
-            quantise(z_rounded, z_codes, z_plane, lo, hi)
-            for t in range(PACK):
-                product(h_acc[t][:, lo:hi], w3_codes, w3_plane, t, z_codes[:, lo:hi], z_plane[:, lo:hi])
+                nc.scalar.activation(planes[:, t, :], y_rows[t][:].indirect(entries(n2_l, lo, hi)), ACT.Copy)
+            return planes
+
+        def add_and_round(planes, lo, hi):
+            rounded = keep.tile([P, PACK * (hi - lo)], BF16, name="z_rounded%d" % lo, tag="z_rounded", align_bytes=64)
+            nc.vector.tensor_tensor(woven(rounded), in_fours(gated[:, :, lo:hi]), in_fours(planes), ALU.add)
+            return rounded
+
+        c1, c2 = CUTS
+        summed = keep.tile([P, PACK, c1], F32, name="summed")
+        for t in range(PACK):
+            nc.vector.tensor_tensor(summed[:, t, :], y_rows[t][:].indirect(entries(n2_l, 0, c1)), gated[:, t, 0:c1], ALU.add)
+        middle = fetch_on_scalar(c1, c2)
+        first_rounded = keep.tile([P, PACK * c1], BF16, name="first_rounded", align_bytes=64)
+        nc.scalar.copy(woven(first_rounded), in_fours(summed[:]))
+        end = fetch_on_scalar(c2, S)
+        third_product(add_and_round(middle, c1, c2), c1, c2)
+        third_product(first_rounded, 0, c1)
+        third_product(add_and_round(end, c2, S), c2, S)
+        for t in range(1, PACK):
+            product(h_acc[t][:], w3_codes, w3_plane, t, z_codes[:], z_plane[:])
 
         top = keep.tile([P, PACK], F32, name="top")
         exp_bias = keep.tile([P, PACK], F32, name="exp_bias")
@@ -194,9 +230,11 @@ def tile_picked_twhgxbelg_none_p_kernel(tc, x_words, x_scales, w1, w2, sl, th, g
         for t in range(PACK):
             logs = h_rows[last][:, S * (t + 1) : S * (t + 2)] if t < last else sg_last[:]
             result = keep.tile([P, S], F32, name="result%d" % t)
-            step = S // 2 if t == last else S
-            for lo in range(0, S, step):
-                cols = slice(lo, lo + step)
+            for lo in range(0, S, HALF):
+                cols = slice(lo, lo + HALF)
                 nc.scalar.activation(logs[:, cols], total[t][:, cols], ACT.Ln)
                 nc.vector.tensor_tensor(result[:, cols], h_rows[t][:, cols], logs[:, cols], ALU.add)
-                nc.sync.dma_start(out_rows[t][:, cols], result[:, cols])
+                if t == last:
+                    nc.sync.dma_start(out_rows[t][:, cols], result[:, cols])
+            if t < last:
+                nc.sync.dma_start(out_rows[t], result[:])

from contextlib import ExitStack

import concourse.mybir as mybir

K, T, S, N, H = 512, 2048, 512, 512, 512
FLOPS = 3 * 2 * 512 * 512 * 512

F32 = mybir.dt.float32
BF16 = mybir.dt.bfloat16
I32 = mybir.dt.int32
U32 = mybir.dt.uint32
U16 = mybir.dt.uint16
U8 = mybir.dt.uint8
FP8X4 = mybir.dt.float8_e4m3fn_x4
ALU = mybir.AluOpType
ACT = mybir.ActivationFunctionType

P = 128
PACK = 4
STRIPE = 16
CUTS = (128, 384)
HALF = 256


def tile_picked_twhgxbelg_none_p_kernel(tc, x_words, x_scales, w1, w2, sl, th, gn, w3, tau, offs, hz, n1, n2, n3, n4, out):
    nc = tc.nc
    with ExitStack() as ctx:
        keep = ctx.enter_context(tc.tile_pool(name="keep", bufs=1))
        psum = ctx.enter_context(tc.psum_pool(name="psum", bufs=1))

        def load_list(src, name):
            tile = keep.tile([P, S // STRIPE], U16, name=name)
            nc.sync.dma_start(tile[:], src)
            return tile

        def entries(tile, lo, hi):
            return tile[:, lo // STRIPE : hi // STRIPE]

        def load_weight(w, name, tag):
            tile = keep.tile([P, PACK * w.shape[1]], F32, name=name, tag=tag, align_bytes=64)
            nc.sync.dma_start(by_row(tile), w.rearrange("(p j) c -> p j c", j=PACK))
            return tile

        def by_row(tile):
            return tile[:].rearrange("p (j c) -> p j c", j=PACK)

        def load_column(vec, name):
            tile = keep.tile([P, PACK], F32, name=name)
            nc.gpsimd.dma_start(tile[:], vec.rearrange("(p t) o -> p (t o)", t=PACK))
            return tile

        def dealt(raw, rounded, first_column):
            lo = first_column // PACK
            hi = lo + raw.shape[1] // (PACK * PACK)
            dst = rounded[:].rearrange("p (t m j) -> p m j t", t=PACK, j=PACK)[:, lo:hi]
            src = raw[:].rearrange("p (j m t) -> p m j t", j=PACK, t=PACK)
            return dst, src

        def quantise(rounded, codes, plane, lo, hi):
            nc.vector.quantize_mx(out=codes[:, lo:hi].bitcast(FP8X4), scales=plane[:, lo:hi], in_=rounded[:, PACK * lo : PACK * hi])

        def product(acc, codes, plane, t, rhs, rhs_plane):
            cols = slice(P * t, P * (t + 1))
            nc.tensor.matmul_mx(out=acc, lhsT=codes[:, cols].bitcast(FP8X4), lhsT_scale=plane[:, cols], rhs=rhs.bitcast(FP8X4), rhs_scale=rhs_plane, start=True, stop=True)

        def weight_tiles(name):
            rounded = keep.tile([P, PACK * H], BF16, name=name + "_rounded", tag=name + "_rounded", align_bytes=64)
            codes = keep.tile([P, H], U32, name=name + "_codes", align_bytes=64)
            plane = keep.tile([P, H], U8, name=name + "_plane", align_bytes=64)
            return rounded, codes, plane

        warm_in = keep.tile([P, 1], F32, name="warm_in")
        warm_out = keep.tile([P, 1], F32, name="warm_out")
        nc.gpsimd.memset(warm_in[:], 0.0)
        nc.scalar.activation(warm_out[:], warm_in[:], ACT.Sigmoid)

        scale_table = keep.tile([P, T], U8, name="scale_table", tag="table_then_w1", align_bytes=64)
        nc.vector.memset(scale_table[:].bitcast(I32), 0)
        hz_plane = keep.tile([P, S], U8, name="hz_plane", align_bytes=64)
        offs_plane = keep.tile([P, S], U8, name="offs_plane", align_bytes=64)
        nc.vector.memset(hz_plane[:].bitcast(I32), 0)
        nc.vector.memset(offs_plane[:].bitcast(I32), 0)
        nc.sync.dma_start(scale_table[0:P:8, :].bitcast(I32), x_scales[0].bitcast(I32))
        hz_l = load_list(hz, "hz_l")
        w2_raw = [load_weight(w2[:, 0:HALF], "w2_raw0", "w2_raw0")]
        offs_l = load_list(offs, "offs_l")
        n1_l = load_list(n1, "n1_l")
        n2_l = load_list(n2, "n2_l")
        n3_l = load_list(n3, "n3_l")
        word_table = keep.tile([P, T], I32, name="word_table", align_bytes=64)
        nc.sync.dma_start(word_table[:], x_words[0].rearrange("p n r -> p (n r)").bitcast(I32))
        w2_raw.append(load_weight(w2[:, HALF:H], "w2_raw1", "w2_raw1"))
        w1_raw = [load_weight(w1[:, 0:HALF], "w1_raw0", "w1_raw0")]
        n4_l = load_list(n4, "n4_l")
        sl_c = load_column(sl, "sl_c")
        th_c = load_column(th, "th_c")
        gn_c = load_column(gn, "gn_c")
        tau_c = load_column(tau, "tau_c")
        sl_th = keep.tile([P, PACK], F32, name="sl_th")
        nc.gpsimd.tensor_tensor(sl_th[:], sl_c[:], th_c[:], ALU.mult)
        sig_bias = keep.tile([P, PACK], F32, name="sig_bias")
        nc.gpsimd.tensor_scalar(sig_bias[:], sl_th[:], -1.0, 0.0, ALU.mult, ALU.add)

        def move_rows(plane, picked):
            for a in range(4):
                nc.sync.dma_start(plane[a:P:32, :].bitcast(I32), picked[8 * a : P : 32, :].bitcast(I32))

        hz_scales = keep.tile([P, S], U8, name="hz_scales", align_bytes=64)
        offs_scales = keep.tile([P, S], U8, name="offs_scales", align_bytes=64)
        nc.vector.tensor_copy(hz_scales[:], scale_table[:].indirect(hz_l[:]))
        move_rows(hz_plane, hz_scales)
        nc.vector.tensor_copy(offs_scales[:], scale_table[:].indirect(offs_l[:]))
        w1_raw.append(load_weight(w1[:, HALF:H], "w1_raw1", "table_then_w1"))
        move_rows(offs_plane, offs_scales)

        hz_words = keep.tile([P, S], U32, name="hz_words", align_bytes=64)
        nc.vector.tensor_copy(hz_words[:], word_table[:].bitcast(U32).indirect(hz_l[:]))
        offs_words = keep.tile([P, S], U32, name="offs_words", align_bytes=64)
        nc.vector.tensor_copy(offs_words[:], word_table[:].bitcast(U32).indirect(offs_l[:]))

        w2_rounded, w2_codes, w2_plane = weight_tiles("w2")
        for u in range(2):
            nc.scalar.copy(*dealt(w2_raw[u], w2_rounded, HALF * u))
        quantise(w2_rounded, w2_codes, w2_plane, 0, P)
        quantise(w2_rounded, w2_codes, w2_plane, P, H)
        w3_raw = load_weight(w3, "w3_raw", "w2_rounded")
        d_acc = [psum.tile([P, S], F32, name="d_acc%d" % t, tag="bank%d" % t) for t in range(PACK)]
        d_rows = w2_raw + w1_raw
        last = PACK - 1
        h_rows = [keep.tile([P, (PACK if t == last else 2) * S], F32, name="h_rows%d" % t) for t in range(PACK)]
        sg_last = keep.tile([P, S], F32, name="sg_last")
        sg = [h_rows[t][:, S : 2 * S] for t in range(last)] + [sg_last[:]]
        for t in range(PACK):
            product(d_acc[t][:], w2_codes, w2_plane, t, hz_words[:], hz_plane[:])

        def sigmoid(t):
            nc.scalar.activation(sg[t], d_rows[t][:].indirect(n1_l[:]), ACT.Sigmoid, bias=sig_bias[:, t : t + 1], scale=sl_c[:, t : t + 1])

        w1_rounded, w1_codes, w1_plane = weight_tiles("w1")
        y_acc = [psum.tile([P, S], F32, name="y_acc%d" % t, tag="bank%d" % (PACK + t)) for t in range(PACK)]
        y_rows = [keep.tile([P, S], F32, name="y_rows%d" % t) for t in range(PACK)]

        nc.scalar.copy(*dealt(w1_raw[0], w1_rounded, 0))
        nc.scalar.copy(d_rows[0][:, 0:S], d_acc[0][:])
        sigmoid(0)
        nc.scalar.copy(d_rows[1][:, 0:S], d_acc[1][:])
        sigmoid(1)
        nc.vector.tensor_copy(*dealt(w1_raw[1], w1_rounded, HALF))
        quantise(w1_rounded, w1_codes, w1_plane, 0, P)
        quantise(w1_rounded, w1_codes, w1_plane, P, H)
        for t in range(PACK):
            product(y_acc[t][:], w1_codes, w1_plane, t, offs_words[:], offs_plane[:])
        nc.scalar.copy(d_rows[2][:, 0:S], d_acc[2][:])
        sigmoid(2)
        nc.scalar.copy(d_rows[3][:, 0:S], d_acc[3][:])
        sigmoid(3)
        for t in range(PACK):
            nc.vector.tensor_scalar(y_rows[t][:], y_acc[t][:], gn_c[:, t : t + 1], -0.5, ALU.mult, ALU.mult)

        w3_rounded, w3_codes, w3_plane = weight_tiles("w3")
        for t in range(PACK):
            nc.gpsimd.tensor_scalar(
                w3_rounded[:, N * t : N * (t + 1)].rearrange("p (m j) -> p m j", j=PACK),
                w3_raw[:].rearrange("p (j m t) -> p t m j", j=PACK, t=PACK)[:, t],
                1.0,
                0.0,
                ALU.mult,
                ALU.add,
            )

        gated = keep.tile([P, PACK, S], F32, name="gated")
        for t in range(PACK):
            nc.vector.scalar_tensor_tensor(gated[:, t, :], y_acc[t][:], gn_c[:, t : t + 1], sg[t], ALU.mult, ALU.mult)
        quantise(w3_rounded, w3_codes, w3_plane, 0, N)
        h_acc = [psum.tile([P, S], F32, name="h_acc%d" % t, tag="bank%d" % t) for t in range(PACK)]

        def woven(rounded):
            return rounded[:].rearrange("p (c i t) -> p c t i", i=4, t=PACK)

        def in_fours(planes):
            return planes.rearrange("p t (c i) -> p c t i", i=4)

        z_codes = keep.tile([P, S], U32, name="z_codes", align_bytes=64)
        z_plane = keep.tile([P, S], U8, name="z_plane", align_bytes=64)

        def third_product(rounded, lo, hi):
            nc.vector.quantize_mx(out=z_codes[:, lo:hi].bitcast(FP8X4), scales=z_plane[:, lo:hi], in_=rounded[:])
            product(h_acc[0][:, lo:hi], w3_codes, w3_plane, 0, z_codes[:, lo:hi], z_plane[:, lo:hi])

        def fetch_on_scalar(lo, hi):
            planes = h_rows[last][:, PACK * lo : PACK * hi].rearrange("p (t c) -> p t c", t=PACK)
            for t in range(PACK):
                nc.scalar.activation(planes[:, t, :], y_rows[t][:].indirect(entries(n2_l, lo, hi)), ACT.Copy)
            return planes

        def add_and_round(planes, lo, hi):
            rounded = keep.tile([P, PACK * (hi - lo)], BF16, name="z_rounded%d" % lo, tag="z_rounded", align_bytes=64)
            nc.vector.tensor_tensor(woven(rounded), in_fours(gated[:, :, lo:hi]), in_fours(planes), ALU.add)
            return rounded

        c1, c2 = CUTS
        summed = keep.tile([P, PACK, c1], F32, name="summed")
        for t in range(PACK):
            nc.vector.tensor_tensor(summed[:, t, :], y_rows[t][:].indirect(entries(n2_l, 0, c1)), gated[:, t, 0:c1], ALU.add)
        middle = fetch_on_scalar(c1, c2)
        first_rounded = keep.tile([P, PACK * c1], BF16, name="first_rounded", align_bytes=64)
        nc.scalar.copy(woven(first_rounded), in_fours(summed[:]))
        end = fetch_on_scalar(c2, S)
        third_product(add_and_round(middle, c1, c2), c1, c2)
        third_product(first_rounded, 0, c1)
        third_product(add_and_round(end, c2, S), c2, S)
        for t in range(1, PACK):
            product(h_acc[t][:], w3_codes, w3_plane, t, z_codes[:], z_plane[:])

        top = keep.tile([P, PACK], F32, name="top")
        exp_bias = keep.tile([P, PACK], F32, name="exp_bias")
        total = [keep.tile([P, S], F32, name="total%d" % t) for t in range(PACK)]
        for t in range(PACK):
            col = slice(t, t + 1)
            nc.vector.tensor_scalar(h_rows[t][:, 0:S], h_acc[t][:], 1.0, None, ALU.mult, ALU.max, accum_out=top[:, col])
            nc.vector.tensor_scalar(exp_bias[:, col], top[:, col], tau_c[:, col], -1.0, ALU.mult, ALU.mult)
        for t in range(PACK):
            col = slice(t, t + 1)
            ea = keep.tile([P, S], F32, name="ea%d" % t)
            ea2 = keep.tile([P, S], F32, name="ea2_%d" % t)
            nc.scalar.activation(ea[:], h_rows[t][:].indirect(n3_l[:]), ACT.Exp, bias=exp_bias[:, col], scale=tau_c[:, col])
            nc.scalar.activation(ea2[:], h_rows[t][:].indirect(n4_l[:]), ACT.Exp, bias=exp_bias[:, col], scale=tau_c[:, col])
            nc.vector.scalar_tensor_tensor(total[t][:], ea[:], 0.25, ea2[:], ALU.add, ALU.add)
        out_rows = out.rearrange("(p t) s -> t p s", t=PACK)
        for t in range(PACK):
            logs = h_rows[last][:, S * (t + 1) : S * (t + 2)] if t < last else sg_last[:]
            result = keep.tile([P, S], F32, name="result%d" % t)
            for lo in range(0, S, HALF):
                cols = slice(lo, lo + HALF)
                nc.scalar.activation(logs[:, cols], total[t][:, cols], ACT.Ln)
                nc.vector.tensor_tensor(result[:, cols], h_rows[t][:, cols], logs[:, cols], ALU.add)
                if t == last:
                    nc.sync.dma_start(out_rows[t][:, cols], result[:, cols])
            if t < last:
                nc.sync.dma_start(out_rows[t], result[:])
